import numpy as np, ml_dtypes
CORES = [37,45,53,61,69,109,117,125]
N = 8
C = 256
SIGN = [[1,1,1,1,1,1,1,1],[1,-1,1,-1,1,-1,1,-1],[1,1,-1,-1,1,1,-1,-1],[1,-1,-1,1,1,-1,-1,1],[1,1,1,1,-1,-1,-1,-1],[1,-1,1,-1,-1,1,-1,1],[1,1,-1,-1,-1,-1,1,1],[1,-1,-1,1,-1,1,1,-1]]
def setup_inputs(rng):
    return {"x": rng.standard_normal((N, 128, C), dtype=np.float32).astype(ml_dtypes.bfloat16)}
def setup_inputs_big(rng):
    d = setup_inputs(rng)
    for k in ("x",): d[k] = (d[k].astype(np.float32) * 1048576.0).astype(d[k].dtype)
    return d
def setup_inputs_small(rng):
    d = setup_inputs(rng)
    for k in ("x",): d[k] = (d[k].astype(np.float32) * (1 / 1048576.0)).astype(d[k].dtype)
    return d
def setup_inputs_apart(rng):
    d = setup_inputs(rng)
    f = (10.0 ** rng.permutation(np.linspace(-1.5, 1.5, N))).astype(np.float32).reshape(N, 1, 1)
    for k in ("x",): d[k] = (d[k].astype(np.float32) * f).astype(d[k].dtype)
    return d
def reference(x):
    X = x.astype(np.float64)
    y = np.stack([sum(SIGN[r][j] * X[j] for j in range(N)) for r in range(N)])
    return {"y": y.astype(ml_dtypes.bfloat16)}

@@ -1,0 +1,135 @@
+from concourse.bass import DstId, RemoteDMATransfer
+from concourse.mybir import AluOpType
+
+C = 256
+G = 4
+NE = 8
+
+SCRATCH = {
+    "xs": ("sbuf", [128, C], "bfloat16"),
+    "zero": ("sbuf", [128, C], "bfloat16"),
+    "nx": ("sbuf", [128, C], "bfloat16"),
+    "land": ("sbuf", [128, G * C], "bfloat16"),
+    "zown": ("sbuf", [128, C], "bfloat16"),
+    "zcross": ("sbuf", [128, C], "bfloat16"),
+    "ys": ("sbuf", [128, C], "bfloat16"),
+}
+SEMAPHORES = ["loaded", "filled", "negated", "sent", "landed", "arrived", "summed", "stored"]
+
+
+def _take(mask, k):
+    out, n, b = 0, 0, 1
+    while n < k and b <= mask:
+        if mask & b:
+            out |= b
+            n += 1
+        b <<= 1
+    assert n == k
+    return out
+
+
+def _plan(T, topo):
+    cores = list(T.cores)
+    S = T.tables["SIGN"]
+    n = len(cores)
+    planes = []
+    for r in range(n):
+        for p in planes:
+            if topo.same_plane(topo.chip(cores[p[0]]), topo.chip(cores[r])):
+                p.append(r)
+                break
+        else:
+            planes.append([r])
+    plane_of = {}
+    for p in planes:
+        for r in p:
+            plane_of[r] = p
+    partner, helper = {}, {}
+    for r in range(n):
+        cand = [p for p in range(n) if plane_of[p] is not plane_of[r]
+                and all(len(set(S[r][j] * S[p][j] for j in q)) == 1 for q in planes)]
+        partner[r] = cand[0]
+        c = cores[r]
+        hs = [h for h in range(topo.CHIPS * topo.CORES_PER_CHIP)
+              if topo.chip(h) == topo.chip(c) and topo.die(h) == topo.die(c) and h not in cores
+              and topo.may_write(h, cores[partner[r]]) and topo.may_write(h, c)]
+        helper[r] = hs[0]
+    return cores, S, plane_of, partner, helper
+
+
+def _dst(topo, c):
+    rid, pid, _ = topo.addr(c)
+    return DstId(rid=rid, pnc=pid)
+
+
+def _rank(g, core, rank, T, topo, plan):
+    cores, S, plane_of, partner, helper = plan
+    sem = T.sem
+    plane = plane_of[rank]
+    k = plane.index(rank)
+    order = plane[k + 1:] + plane[:k] + [rank]
+    sign = {r: S[r][plane[0]] * S[r][rank] for r in order}
+    pos = [r for r in order if sign[r] > 0]
+    neg = [r for r in order if sign[r] < 0]
+
+    g.sync.dma_start(T.xs[:], T.x[:]).then_inc(sem.loaded, 16)
+    if neg:
+        g.vector.memset(T.zero[:], 0.0).then_inc(sem.filled, 1)
+        g.vector.wait_ge(sem.filled, 1)
+        g.vector.wait_ge(sem.loaded, 16)
+        g.vector.tensor_tensor(T.nx[:], T.zero[:], T.xs[:], AluOpType.subtract).then_inc(sem.negated, 1)
+
+    def send(src, to):
+        m = topo.mask(core, helper[to[0]])
+        for r in to:
+            m &= topo.mask(core, helper[r])
+        g.remote_dma_fused([RemoteDMATransfer(
+            dst_ids=[_dst(topo, helper[r]) for r in to], dma_engine_mask=_take(m, NE), remote_sem=sem.landed,
+            srcs=[src[:]], dsts=[T.land[:, k * C:(k + 1) * C] for r in to], alu_op=0)], local_sem=sem.sent)
+        return NE
+
+    g.wait_ge(sem.loaded, 16)
+    left = send(T.xs, pos)
+    if neg:
+        g.wait_ge(sem.negated, 1)
+        left += send(T.nx, neg)
+
+    a = S[rank][plane[0]]
+    c = S[rank][plane_of[partner[rank]][0]]
+    assert a > 0 or c > 0
+    g.vector.wait_ge(sem.arrived, 2 * NE)
+    if a > 0 and c > 0:
+        op = g.vector.tensor_tensor(T.ys[:], T.zown[:], T.zcross[:], AluOpType.add)
+    elif a > 0:
+        op = g.vector.tensor_tensor(T.ys[:], T.zown[:], T.zcross[:], AluOpType.subtract)
+    else:
+        op = g.vector.tensor_tensor(T.ys[:], T.zcross[:], T.zown[:], AluOpType.subtract)
+    op.then_inc(sem.summed, 1)
+    g.sync.wait_ge(sem.summed, 1)
+    g.sync.dma_start(T.y[:], T.ys[:]).then_inc(sem.stored, 16)
+    g.sync.wait_ge(sem.stored, 16)
+    g.wait_ge(sem.sent, left)
+
+
+def _helper(g, core, rank, T, topo, plan):
+    cores, S, plane_of, partner, helper = plan
+    sem = T.sem
+    own, far = cores[rank], cores[partner[rank]]
+    m = _take(topo.mask(core, far) & topo.mask(core, own), NE)
+    g.wait_ge(sem.landed, G * NE)
+    g.remote_dma_fused([RemoteDMATransfer(
+        dst_ids=[_dst(topo, far), _dst(topo, own)], dma_engine_mask=m, remote_sem=sem.arrived,
+        srcs=[T.land[:, i * C:(i + 1) * C] for i in range(G)], dsts=[T.zcross[:], T.zown[:]], alu_op=1)],
+        local_sem=sem.sent)
+    g.wait_ge(sem.sent, NE)
+
+
+def rank_program(g, core, T, topo):
+    plan = _plan(T, topo)
+    rank = T.rank_of(core)
+    if rank is not None:
+        _rank(g, core, rank, T, topo, plan)
+        return
+    for r, h in plan[4].items():
+        if h == core:
+            _helper(g, core, r, T, topo, plan)

@@ -3,29 +3,31 @@ from concourse.mybir import AluOpType
 
 C = 256
 G = 4
+HPC = 2
+Q = 4
+W = C // Q
+RQ = 128 // Q
 NE = 8
 
 SCRATCH = {
+    "xd": ("dram", [Q, 128, W], "bfloat16"),
     "xs": ("sbuf", [128, C], "bfloat16"),
-    "zero": ("sbuf", [128, C], "bfloat16"),
-    "nx": ("sbuf", [128, C], "bfloat16"),
-    "land": ("sbuf", [128, G * C], "bfloat16"),
+    "nxs": ("sbuf", [128, C], "bfloat16"),
+    "nxd": ("dram", [Q, 128, W], "bfloat16"),
+    "lande": ("dram", [G, 128, W], "bfloat16"),
+    "landl": ("dram", [G, 128, W], "bfloat16"),
     "zown": ("sbuf", [128, C], "bfloat16"),
     "zcross": ("sbuf", [128, C], "bfloat16"),
     "ys": ("sbuf", [128, C], "bfloat16"),
 }
-SEMAPHORES = ["loaded", "filled", "negated", "sent", "landed", "arrived", "summed", "stored"]
+SEMAPHORES = ["loaded", "loaded2", "negated", "negstored", "sent", "landede", "landedl",
+              "arre", "arrl", "sume", "suml", "stored0", "stored1"]
 
 
-def _take(mask, k):
-    out, n, b = 0, 0, 1
-    while n < k and b <= mask:
-        if mask & b:
-            out |= b
-            n += 1
-        b <<= 1
-    assert n == k
-    return out
+def _take(mask, k, skip=0):
+    bits = [1 << i for i in range(mask.bit_length()) if (mask >> i) & 1]
+    assert len(bits) >= skip + k
+    return sum(bits[skip:skip + k])
 
 
 def _plan(T, topo):
@@ -53,7 +55,8 @@ def _plan(T, topo):
         hs = [h for h in range(topo.CHIPS * topo.CORES_PER_CHIP)
               if topo.chip(h) == topo.chip(c) and topo.die(h) == topo.die(c) and h not in cores
               and topo.may_write(h, cores[partner[r]]) and topo.may_write(h, c)]
-        helper[r] = hs[0]
+        assert len(hs) >= HPC
+        helper[r] = hs[:HPC]
     return cores, S, plane_of, partner, helper
 
 
@@ -72,56 +75,72 @@ def _rank(g, core, rank, T, topo, plan):
     pos = [r for r in order if sign[r] > 0]
     neg = [r for r in order if sign[r] < 0]
 
-    g.sync.dma_start(T.xs[:], T.x[:]).then_inc(sem.loaded, 16)
+    g.sync.dma_start(T.xd[:], T.x[:]).then_inc(sem.loaded, 16)
     if neg:
-        g.vector.memset(T.zero[:], 0.0).then_inc(sem.filled, 1)
-        g.vector.wait_ge(sem.filled, 1)
-        g.vector.wait_ge(sem.loaded, 16)
-        g.vector.tensor_tensor(T.nx[:], T.zero[:], T.xs[:], AluOpType.subtract).then_inc(sem.negated, 1)
+        g.scalar.dma_start(T.xs[:], T.x[:]).then_inc(sem.loaded2, 16)
+        g.vector.wait_ge(sem.loaded2, 16)
+        g.vector.tensor_scalar(T.nxs[:], T.xs[:], -1.0, None, AluOpType.mult).then_inc(sem.negated, 1)
+        g.scalar.wait_ge(sem.negated, 1)
+        g.scalar.dma_start(T.nxd[:], T.nxs[:]).then_inc(sem.negstored, 16)
 
-    def send(src, to):
-        m = topo.mask(core, helper[to[0]])
-        for r in to:
-            m &= topo.mask(core, helper[r])
+    m = -1
+    for r in order:
+        for h in helper[r]:
+            m &= topo.mask(core, h)
+    ne = NE // HPC
+
+    def send(src, to, half):
+        land, rsem = ((T.lande, sem.landede), (T.landl, sem.landedl))[half]
         g.remote_dma_fused([RemoteDMATransfer(
-            dst_ids=[_dst(topo, helper[r]) for r in to], dma_engine_mask=_take(m, NE), remote_sem=sem.landed,
-            srcs=[src[:]], dsts=[T.land[:, k * C:(k + 1) * C] for r in to], alu_op=0)], local_sem=sem.sent)
+            dst_ids=[_dst(topo, helper[r][t]) for r in to], dma_engine_mask=_take(m, ne, t * ne), remote_sem=rsem,
+            srcs=[src[half * HPC + t]], dsts=[land[k] for r in to], alu_op=0) for t in range(HPC)], local_sem=sem.sent)
         return NE
 
+    left = 0
     g.wait_ge(sem.loaded, 16)
-    left = send(T.xs, pos)
-    if neg:
-        g.wait_ge(sem.negated, 1)
-        left += send(T.nx, neg)
+    for half in range(2):
+        left += send(T.xd, pos, half)
+        if neg:
+            if half == 0:
+                g.wait_ge(sem.negstored, 16)
+            left += send(T.nxd, neg, half)
 
     a = S[rank][plane[0]]
     c = S[rank][plane_of[partner[rank]][0]]
     assert a > 0 or c > 0
-    g.vector.wait_ge(sem.arrived, 2 * NE)
-    if a > 0 and c > 0:
-        op = g.vector.tensor_tensor(T.ys[:], T.zown[:], T.zcross[:], AluOpType.add)
-    elif a > 0:
-        op = g.vector.tensor_tensor(T.ys[:], T.zown[:], T.zcross[:], AluOpType.subtract)
-    else:
-        op = g.vector.tensor_tensor(T.ys[:], T.zcross[:], T.zown[:], AluOpType.subtract)
-    op.then_inc(sem.summed, 1)
-    g.sync.wait_ge(sem.summed, 1)
-    g.sync.dma_start(T.y[:], T.ys[:]).then_inc(sem.stored, 16)
-    g.sync.wait_ge(sem.stored, 16)
+    H = C // 2
+    for half, arr, done in ((0, sem.arre, sem.sume), (1, sem.arrl, sem.suml)):
+        o = slice(half * H, (half + 1) * H)
+        g.vector.wait_ge(arr, 2 * HPC * NE)
+        if a > 0 and c > 0:
+            op = g.vector.tensor_tensor(T.ys[:, o], T.zown[:, o], T.zcross[:, o], AluOpType.add)
+        elif a > 0:
+            op = g.vector.tensor_tensor(T.ys[:, o], T.zown[:, o], T.zcross[:, o], AluOpType.subtract)
+        else:
+            op = g.vector.tensor_tensor(T.ys[:, o], T.zcross[:, o], T.zown[:, o], AluOpType.subtract)
+        op.then_inc(done, 1)
+        for t, (qu, st) in enumerate(((g.sync, sem.stored0), (g.scalar, sem.stored1))):
+            q = half * HPC + t
+            qu.wait_ge(done, 1)
+            qu.dma_start(T.y[q * RQ:(q + 1) * RQ, :], T.ys[:, q * W:(q + 1) * W]).then_inc(st, 16)
+    g.sync.wait_ge(sem.stored0, 32)
+    g.scalar.wait_ge(sem.stored1, 32)
     g.wait_ge(sem.sent, left)
 
 
-def _helper(g, core, rank, T, topo, plan):
+def _helper(g, core, rank, t, T, topo, plan):
     cores, S, plane_of, partner, helper = plan
     sem = T.sem
     own, far = cores[rank], cores[partner[rank]]
     m = _take(topo.mask(core, far) & topo.mask(core, own), NE)
-    g.wait_ge(sem.landed, G * NE)
-    g.remote_dma_fused([RemoteDMATransfer(
-        dst_ids=[_dst(topo, far), _dst(topo, own)], dma_engine_mask=m, remote_sem=sem.arrived,
-        srcs=[T.land[:, i * C:(i + 1) * C] for i in range(G)], dsts=[T.zcross[:], T.zown[:]], alu_op=1)],
-        local_sem=sem.sent)
-    g.wait_ge(sem.sent, NE)
+    for half, land, lsem, arr in ((0, T.lande, sem.landede, sem.arre), (1, T.landl, sem.landedl, sem.arrl)):
+        q = half * HPC + t
+        g.wait_ge(lsem, G * (NE // HPC))
+        g.remote_dma_fused([RemoteDMATransfer(
+            dst_ids=[_dst(topo, far), _dst(topo, own)], dma_engine_mask=m, remote_sem=arr,
+            srcs=[land[i] for i in range(G)],
+            dsts=[T.zcross[:, q * W:(q + 1) * W], T.zown[:, q * W:(q + 1) * W]], alu_op=1)], local_sem=sem.sent)
+    g.wait_ge(sem.sent, 2 * NE)
 
 
 def rank_program(g, core, T, topo):
@@ -130,6 +149,6 @@ def rank_program(g, core, T, topo):
     if rank is not None:
         _rank(g, core, rank, T, topo, plan)
         return
-    for r, h in plan[4].items():
-        if h == core:
-            _helper(g, core, r, T, topo, plan)
+    for r, hs in plan[4].items():
+        if core in hs:
+            _helper(g, core, r, hs.index(core), T, topo, plan)

@@ -4,24 +4,30 @@ from concourse.mybir import AluOpType
 C = 256
 G = 4
 HPC = 2
-Q = 4
-W = C // Q
-RQ = 128 // Q
+H = C // 2
+W = H // HPC
+RH = 64
+RQ = RH // HPC
 NE = 8
 
 SCRATCH = {
-    "xd": ("dram", [Q, 128, W], "bfloat16"),
-    "xs": ("sbuf", [128, C], "bfloat16"),
-    "nxs": ("sbuf", [128, C], "bfloat16"),
-    "nxd": ("dram", [Q, 128, W], "bfloat16"),
-    "lande": ("dram", [G, 128, W], "bfloat16"),
+    "xe": ("dram", [128, H], "bfloat16"),
+    "xl": ("dram", [HPC, 128, W], "bfloat16"),
+    "xs": ("sbuf", [128, H], "bfloat16"),
+    "nxs": ("sbuf", [128, H], "bfloat16"),
+    "nxl": ("dram", [HPC, 128, W], "bfloat16"),
+    "landh": ("dram", [G, 128, H], "bfloat16"),
     "landl": ("dram", [G, 128, W], "bfloat16"),
-    "zown": ("sbuf", [128, C], "bfloat16"),
-    "zcross": ("sbuf", [128, C], "bfloat16"),
-    "ys": ("sbuf", [128, C], "bfloat16"),
+    "eo": ("sbuf", [128, HPC * H], "bfloat16"),
+    "ec": ("sbuf", [128, HPC * H], "bfloat16"),
+    "ew": ("sbuf", [128, HPC * H], "bfloat16"),
+    "ye": ("sbuf", [128, H], "bfloat16"),
+    "zo": ("sbuf", [128, H], "bfloat16"),
+    "zc": ("sbuf", [128, H], "bfloat16"),
+    "yl": ("sbuf", [128, H], "bfloat16"),
 }
-SEMAPHORES = ["loaded", "loaded2", "negated", "negstored", "sent", "landede", "landedl",
-              "arre", "arrl", "sume", "suml", "stored0", "stored1"]
+SEMAPHORES = ["loaded", "loadedl", "loaded2", "negated", "negstored", "sent", "landede", "landedl",
+              "arre", "arrl", "mid", "sume", "suml", "stored0", "stored1"]
 
 
 def _take(mask, k, skip=0):
@@ -46,7 +52,7 @@ def _plan(T, topo):
     for p in planes:
         for r in p:
             plane_of[r] = p
-    partner, helper = {}, {}
+    partner, helper, pat = {}, {}, {}
     for r in range(n):
         cand = [p for p in range(n) if plane_of[p] is not plane_of[r]
                 and all(len(set(S[r][j] * S[p][j] for j in q)) == 1 for q in planes)]
@@ -57,7 +63,14 @@ def _plan(T, topo):
               and topo.may_write(h, cores[partner[r]]) and topo.may_write(h, c)]
         assert len(hs) >= HPC
         helper[r] = hs[:HPC]
-    return cores, S, plane_of, partner, helper
+        pat[r] = tuple(S[r][plane_of[r][0]] * S[r][j] for j in plane_of[r])
+    return cores, S, plane_of, partner, helper, pat
+
+
+def _part(u, k):
+    if min(u) > 0:
+        return 0 if k < G // 2 else 1
+    return 0 if u[k] > 0 else 1
 
 
 def _dst(topo, c):
@@ -65,23 +78,32 @@ def _dst(topo, c):
     return DstId(rid=rid, pnc=pid)
 
 
+def _combine(g, out, a, za, c, zc):
+    assert a > 0 or c > 0
+    if a > 0 and c > 0:
+        return g.vector.tensor_tensor(out, za, zc, AluOpType.add)
+    if a > 0:
+        return g.vector.tensor_tensor(out, za, zc, AluOpType.subtract)
+    return g.vector.tensor_tensor(out, zc, za, AluOpType.subtract)
+
+
 def _rank(g, core, rank, T, topo, plan):
-    cores, S, plane_of, partner, helper = plan
+    cores, S, plane_of, partner, helper, pat = plan
     sem = T.sem
     plane = plane_of[rank]
     k = plane.index(rank)
     order = plane[k + 1:] + plane[:k] + [rank]
-    sign = {r: S[r][plane[0]] * S[r][rank] for r in order}
-    pos = [r for r in order if sign[r] > 0]
-    neg = [r for r in order if sign[r] < 0]
+    pos = [r for r in order if pat[r][k] > 0]
+    neg = [r for r in order if pat[r][k] < 0]
 
-    g.sync.dma_start(T.xd[:], T.x[:]).then_inc(sem.loaded, 16)
+    g.sync.dma_start(T.xe[:], T.x[0:RH, :]).then_inc(sem.loaded, 16)
     if neg:
-        g.scalar.dma_start(T.xs[:], T.x[:]).then_inc(sem.loaded2, 16)
+        g.scalar.dma_start(T.xs[:], T.x[RH:2 * RH, :]).then_inc(sem.loaded2, 16)
         g.vector.wait_ge(sem.loaded2, 16)
         g.vector.tensor_scalar(T.nxs[:], T.xs[:], -1.0, None, AluOpType.mult).then_inc(sem.negated, 1)
         g.scalar.wait_ge(sem.negated, 1)
-        g.scalar.dma_start(T.nxd[:], T.nxs[:]).then_inc(sem.negstored, 16)
+        g.scalar.dma_start(T.nxl[:], T.nxs[:]).then_inc(sem.negstored, 16)
+    g.sync.dma_start(T.xl[:], T.x[RH:2 * RH, :]).then_inc(sem.loadedl, 16)
 
     m = -1
     for r in order:
@@ -89,57 +111,62 @@ def _rank(g, core, rank, T, topo, plan):
             m &= topo.mask(core, h)
     ne = NE // HPC
 
-    def send(src, to, half):
-        land, rsem = ((T.lande, sem.landede), (T.landl, sem.landedl))[half]
+    g.wait_ge(sem.loaded, 16)
+    g.remote_dma_fused([RemoteDMATransfer(
+        dst_ids=[_dst(topo, helper[r][_part(pat[r], k)]) for r in order], dma_engine_mask=_take(m, NE),
+        remote_sem=sem.landede, srcs=[T.xe[:]], dsts=[T.landh[k] for r in order], alu_op=0)], local_sem=sem.sent)
+    left = NE
+
+    def send(src, to):
         g.remote_dma_fused([RemoteDMATransfer(
-            dst_ids=[_dst(topo, helper[r][t]) for r in to], dma_engine_mask=_take(m, ne, t * ne), remote_sem=rsem,
-            srcs=[src[half * HPC + t]], dsts=[land[k] for r in to], alu_op=0) for t in range(HPC)], local_sem=sem.sent)
+            dst_ids=[_dst(topo, helper[r][t]) for r in to], dma_engine_mask=_take(m, ne, t * ne),
+            remote_sem=sem.landedl, srcs=[src[t]], dsts=[T.landl[k] for r in to], alu_op=0)
+            for t in range(HPC)], local_sem=sem.sent)
         return NE
 
-    left = 0
-    g.wait_ge(sem.loaded, 16)
-    for half in range(2):
-        left += send(T.xd, pos, half)
-        if neg:
-            if half == 0:
-                g.wait_ge(sem.negstored, 16)
-            left += send(T.nxd, neg, half)
+    g.wait_ge(sem.loadedl, 16)
+    left += send(T.xl, pos)
+    if neg:
+        g.wait_ge(sem.negstored, 16)
+        left += send(T.nxl, neg)
 
     a = S[rank][plane[0]]
     c = S[rank][plane_of[partner[rank]][0]]
-    assert a > 0 or c > 0
-    H = C // 2
-    for half, arr, done in ((0, sem.arre, sem.sume), (1, sem.arrl, sem.suml)):
-        o = slice(half * H, (half + 1) * H)
-        g.vector.wait_ge(arr, 2 * HPC * NE)
-        if a > 0 and c > 0:
-            op = g.vector.tensor_tensor(T.ys[:, o], T.zown[:, o], T.zcross[:, o], AluOpType.add)
-        elif a > 0:
-            op = g.vector.tensor_tensor(T.ys[:, o], T.zown[:, o], T.zcross[:, o], AluOpType.subtract)
-        else:
-            op = g.vector.tensor_tensor(T.ys[:, o], T.zcross[:, o], T.zown[:, o], AluOpType.subtract)
-        op.then_inc(done, 1)
-        for t, (qu, st) in enumerate(((g.sync, sem.stored0), (g.scalar, sem.stored1))):
-            q = half * HPC + t
-            qu.wait_ge(done, 1)
-            qu.dma_start(T.y[q * RQ:(q + 1) * RQ, :], T.ys[:, q * W:(q + 1) * W]).then_inc(st, 16)
+    sg = 1 if min(pat[rank]) > 0 else -1
+    assert sg == (1 if min(pat[partner[rank]]) > 0 else -1)
+    g.vector.wait_ge(sem.arre, 2 * HPC * NE)
+    _combine(g, T.ew[:], a, T.eo[:], c, T.ec[:]).then_inc(sem.mid, 1)
+    g.vector.wait_ge(sem.mid, 1)
+    _combine(g, T.ye[:], 1, T.ew[:, 0:H], sg, T.ew[:, H:2 * H]).then_inc(sem.sume, 1)
+    g.sync.wait_ge(sem.sume, 1)
+    g.sync.dma_start(T.y[0:RH, :], T.ye[:]).then_inc(sem.stored0, 16)
+
+    g.vector.wait_ge(sem.arrl, 2 * HPC * NE)
+    _combine(g, T.yl[:], a, T.zo[:], c, T.zc[:]).then_inc(sem.suml, 1)
+    for t, (qu, st) in enumerate(((g.sync, sem.stored0), (g.scalar, sem.stored1))):
+        qu.wait_ge(sem.suml, 1)
+        qu.dma_start(T.y[RH + t * RQ:RH + (t + 1) * RQ, :], T.yl[:, t * W:(t + 1) * W]).then_inc(st, 16)
     g.sync.wait_ge(sem.stored0, 32)
-    g.scalar.wait_ge(sem.stored1, 32)
+    g.scalar.wait_ge(sem.stored1, 16)
     g.wait_ge(sem.sent, left)
 
 
 def _helper(g, core, rank, t, T, topo, plan):
-    cores, S, plane_of, partner, helper = plan
+    cores, S, plane_of, partner, helper, pat = plan
     sem = T.sem
     own, far = cores[rank], cores[partner[rank]]
+    to = [_dst(topo, far), _dst(topo, own)]
     m = _take(topo.mask(core, far) & topo.mask(core, own), NE)
-    for half, land, lsem, arr in ((0, T.lande, sem.landede, sem.arre), (1, T.landl, sem.landedl, sem.arrl)):
-        q = half * HPC + t
-        g.wait_ge(lsem, G * (NE // HPC))
-        g.remote_dma_fused([RemoteDMATransfer(
-            dst_ids=[_dst(topo, far), _dst(topo, own)], dma_engine_mask=m, remote_sem=arr,
-            srcs=[land[i] for i in range(G)],
-            dsts=[T.zcross[:, q * W:(q + 1) * W], T.zown[:, q * W:(q + 1) * W]], alu_op=1)], local_sem=sem.sent)
+    mine = [k for k in range(G) if _part(pat[rank], k) == t]
+    assert len(mine) >= 2
+    g.wait_ge(sem.landede, len(mine) * NE)
+    g.remote_dma_fused([RemoteDMATransfer(
+        dst_ids=to, dma_engine_mask=m, remote_sem=sem.arre, srcs=[T.landh[k] for k in mine],
+        dsts=[T.ec[:, t * H:(t + 1) * H], T.eo[:, t * H:(t + 1) * H]], alu_op=1)], local_sem=sem.sent)
+    g.wait_ge(sem.landedl, G * (NE // HPC))
+    g.remote_dma_fused([RemoteDMATransfer(
+        dst_ids=to, dma_engine_mask=m, remote_sem=sem.arrl, srcs=[T.landl[k] for k in range(G)],
+        dsts=[T.zc[:, t * W:(t + 1) * W], T.zo[:, t * W:(t + 1) * W]], alu_op=1)], local_sem=sem.sent)
     g.wait_ge(sem.sent, 2 * NE)
 
 

from concourse.bass import DstId, RemoteDMATransfer
from concourse.mybir import AluOpType

C = 256
G = 4
HPC = 2
H = C // 2
W = H // HPC
RH = 64
RQ = RH // HPC
NE = 8

SCRATCH = {
    "xe": ("dram", [128, H], "bfloat16"),
    "xl": ("dram", [HPC, 128, W], "bfloat16"),
    "xs": ("sbuf", [128, H], "bfloat16"),
    "nxs": ("sbuf", [128, H], "bfloat16"),
    "nxl": ("dram", [HPC, 128, W], "bfloat16"),
    "landh": ("dram", [G, 128, H], "bfloat16"),
    "landl": ("dram", [G, 128, W], "bfloat16"),
    "eo": ("sbuf", [128, HPC * H], "bfloat16"),
    "ec": ("sbuf", [128, HPC * H], "bfloat16"),
    "ew": ("sbuf", [128, HPC * H], "bfloat16"),
    "ye": ("sbuf", [128, H], "bfloat16"),
    "zo": ("sbuf", [128, H], "bfloat16"),
    "zc": ("sbuf", [128, H], "bfloat16"),
    "yl": ("sbuf", [128, H], "bfloat16"),
}
SEMAPHORES = ["loaded", "loadedl", "loaded2", "negated", "negstored", "sent", "landede", "landedl",
              "arre", "arrl", "mid", "sume", "suml", "stored0", "stored1"]


def _take(mask, k, skip=0):
    bits = [1 << i for i in range(mask.bit_length()) if (mask >> i) & 1]
    assert len(bits) >= skip + k
    return sum(bits[skip:skip + k])


def _plan(T, topo):
    cores = list(T.cores)
    S = T.tables["SIGN"]
    n = len(cores)
    planes = []
    for r in range(n):
        for p in planes:
            if topo.same_plane(topo.chip(cores[p[0]]), topo.chip(cores[r])):
                p.append(r)
                break
        else:
            planes.append([r])
    plane_of = {}
    for p in planes:
        for r in p:
            plane_of[r] = p
    partner, helper, pat = {}, {}, {}
    for r in range(n):
        cand = [p for p in range(n) if plane_of[p] is not plane_of[r]
                and all(len(set(S[r][j] * S[p][j] for j in q)) == 1 for q in planes)]
        partner[r] = cand[0]
        c = cores[r]
        hs = [h for h in range(topo.CHIPS * topo.CORES_PER_CHIP)
              if topo.chip(h) == topo.chip(c) and topo.die(h) == topo.die(c) and h not in cores
              and topo.may_write(h, cores[partner[r]]) and topo.may_write(h, c)]
        assert len(hs) >= HPC
        helper[r] = hs[:HPC]
        pat[r] = tuple(S[r][plane_of[r][0]] * S[r][j] for j in plane_of[r])
    return cores, S, plane_of, partner, helper, pat


def _part(u, k):
    if min(u) > 0:
        return 0 if k < G // 2 else 1
    return 0 if u[k] > 0 else 1


def _dst(topo, c):
    rid, pid, _ = topo.addr(c)
    return DstId(rid=rid, pnc=pid)


def _combine(g, out, a, za, c, zc):
    assert a > 0 or c > 0
    if a > 0 and c > 0:
        return g.vector.tensor_tensor(out, za, zc, AluOpType.add)
    if a > 0:
        return g.vector.tensor_tensor(out, za, zc, AluOpType.subtract)
    return g.vector.tensor_tensor(out, zc, za, AluOpType.subtract)


def _rank(g, core, rank, T, topo, plan):
    cores, S, plane_of, partner, helper, pat = plan
    sem = T.sem
    plane = plane_of[rank]
    k = plane.index(rank)
    order = plane[k + 1:] + plane[:k] + [rank]
    pos = [r for r in order if pat[r][k] > 0]
    neg = [r for r in order if pat[r][k] < 0]

    g.sync.dma_start(T.xe[:], T.x[0:RH, :]).then_inc(sem.loaded, 16)
    if neg:
        g.scalar.dma_start(T.xs[:], T.x[RH:2 * RH, :]).then_inc(sem.loaded2, 16)
        g.vector.wait_ge(sem.loaded2, 16)
        g.vector.tensor_scalar(T.nxs[:], T.xs[:], -1.0, None, AluOpType.mult).then_inc(sem.negated, 1)
        g.scalar.wait_ge(sem.negated, 1)
        g.scalar.dma_start(T.nxl[:], T.nxs[:]).then_inc(sem.negstored, 16)
    g.sync.dma_start(T.xl[:], T.x[RH:2 * RH, :]).then_inc(sem.loadedl, 16)

    m = -1
    for r in order:
        for h in helper[r]:
            m &= topo.mask(core, h)
    ne = NE // HPC

    g.wait_ge(sem.loaded, 16)
    g.remote_dma_fused([RemoteDMATransfer(
        dst_ids=[_dst(topo, helper[r][_part(pat[r], k)]) for r in order], dma_engine_mask=_take(m, NE),
        remote_sem=sem.landede, srcs=[T.xe[:]], dsts=[T.landh[k] for r in order], alu_op=0)], local_sem=sem.sent)
    left = NE

    def send(src, to):
        g.remote_dma_fused([RemoteDMATransfer(
            dst_ids=[_dst(topo, helper[r][t]) for r in to], dma_engine_mask=_take(m, ne, t * ne),
            remote_sem=sem.landedl, srcs=[src[t]], dsts=[T.landl[k] for r in to], alu_op=0)
            for t in range(HPC)], local_sem=sem.sent)
        return NE

    g.wait_ge(sem.loadedl, 16)
    left += send(T.xl, pos)
    if neg:
        g.wait_ge(sem.negstored, 16)
        left += send(T.nxl, neg)

    a = S[rank][plane[0]]
    c = S[rank][plane_of[partner[rank]][0]]
    sg = 1 if min(pat[rank]) > 0 else -1
    assert sg == (1 if min(pat[partner[rank]]) > 0 else -1)
    g.vector.wait_ge(sem.arre, 2 * HPC * NE)
    _combine(g, T.ew[:], a, T.eo[:], c, T.ec[:]).then_inc(sem.mid, 1)
    g.vector.wait_ge(sem.mid, 1)
    _combine(g, T.ye[:], 1, T.ew[:, 0:H], sg, T.ew[:, H:2 * H]).then_inc(sem.sume, 1)
    g.sync.wait_ge(sem.sume, 1)
    g.sync.dma_start(T.y[0:RH, :], T.ye[:]).then_inc(sem.stored0, 16)

    g.vector.wait_ge(sem.arrl, 2 * HPC * NE)
    _combine(g, T.yl[:], a, T.zo[:], c, T.zc[:]).then_inc(sem.suml, 1)
    for t, (qu, st) in enumerate(((g.sync, sem.stored0), (g.scalar, sem.stored1))):
        qu.wait_ge(sem.suml, 1)
        qu.dma_start(T.y[RH + t * RQ:RH + (t + 1) * RQ, :], T.yl[:, t * W:(t + 1) * W]).then_inc(st, 16)
    g.sync.wait_ge(sem.stored0, 32)
    g.scalar.wait_ge(sem.stored1, 16)
    g.wait_ge(sem.sent, left)


def _helper(g, core, rank, t, T, topo, plan):
    cores, S, plane_of, partner, helper, pat = plan
    sem = T.sem
    own, far = cores[rank], cores[partner[rank]]
    to = [_dst(topo, far), _dst(topo, own)]
    m = _take(topo.mask(core, far) & topo.mask(core, own), NE)
    mine = [k for k in range(G) if _part(pat[rank], k) == t]
    assert len(mine) >= 2
    g.wait_ge(sem.landede, len(mine) * NE)
    g.remote_dma_fused([RemoteDMATransfer(
        dst_ids=to, dma_engine_mask=m, remote_sem=sem.arre, srcs=[T.landh[k] for k in mine],
        dsts=[T.ec[:, t * H:(t + 1) * H], T.eo[:, t * H:(t + 1) * H]], alu_op=1)], local_sem=sem.sent)
    g.wait_ge(sem.landedl, G * (NE // HPC))
    g.remote_dma_fused([RemoteDMATransfer(
        dst_ids=to, dma_engine_mask=m, remote_sem=sem.arrl, srcs=[T.landl[k] for k in range(G)],
        dsts=[T.zc[:, t * W:(t + 1) * W], T.zo[:, t * W:(t + 1) * W]], alu_op=1)], local_sem=sem.sent)
    g.wait_ge(sem.sent, 2 * NE)


def rank_program(g, core, T, topo):
    plan = _plan(T, topo)
    rank = T.rank_of(core)
    if rank is not None:
        _rank(g, core, rank, T, topo, plan)
        return
    for r, hs in plan[4].items():
        if core in hs:
            _helper(g, core, r, hs.index(core), T, topo, plan)
